import numpy as np
import ml_dtypes


def mxq(x, axis, fmt="e4m3"):
    dtype, down = {"e4m3": (ml_dtypes.float8_e4m3fn, 7), "e5m2": (ml_dtypes.float8_e5m2, 14)}[fmt]
    v = np.moveaxis(np.asarray(x, np.float32).astype(ml_dtypes.bfloat16).astype(np.float64), axis, -1)
    blocks = v.reshape(v.shape[:-1] + (-1, 32))
    amax = np.abs(blocks).max(-1, keepdims=True)
    byte = np.maximum(np.where(amax > 0, np.frexp(amax)[1] - 1 + 127, 0) - down, 1)
    scale = np.exp2(byte - 127.0)
    codes = (blocks / scale).astype(np.float32).astype(dtype).astype(np.float64)
    return np.moveaxis((codes * scale).reshape(v.shape), -1, axis)


WIDE = False


def mx_kscale(k):
    if not WIDE:
        return np.ones(k)
    levels = np.array([10, -10, 5, -5, 0])
    if k % 512:
        return np.exp2(np.random.permutation(np.resize(levels, k // 32))).repeat(32)
    a = np.empty((k // 512, 16))
    for p in range(k // 512):
        a[p, :8] = np.random.permutation(np.resize(levels, 8))
        for g in range(8):
            far = levels[np.abs(levels - a[p, g]) >= 10]
            a[p, g + 8] = far[np.random.randint(len(far))]
    return np.exp2(a.ravel()).repeat(32)


def f64(x):
    return np.asarray(x).astype(np.float64)


def striped(idx):
    return np.tile(idx.reshape(-1, 16).T, (8, 1)).astype(np.uint16)


def unstriped(offs):
    return offs[:16].T.reshape(-1).astype(np.int64)


def relu(v):
    return np.maximum(v, 0.0)


K, T, S, V, H, N = 512, 1024, 512, 1024, 512, 128
P = 2 ** 7


def setup_inputs():
    n = np.random.standard_normal
    s = mx_kscale(K)[:, None]
    u = mx_kscale(H)
    return {
        "xT": (n((K, T)) * s).astype(np.float32),
        "w1": (n((K, H)) / np.sqrt(K) / s * u).astype(np.float32),
        "w2": (n((H, N)) / np.sqrt(H) / u[:, None]).astype(np.float32),
        "gate": np.tile(np.random.uniform(0.5, 1.5, S), (P, 1)).astype(np.float32),
        "offs": striped(np.random.permutation(T)[:S]),
        "pos1": striped(np.random.permutation(V)[:S]),
    }


def reference(xT, w1, w2, gate, offs, pos1):
    h = relu(mxq(f64(w1), 0, "e4m3").T @ mxq(f64(xT)[:, unstriped(offs)], 0, "e4m3"))
    z = np.zeros((H, V))
    z[:, unstriped(pos1)] = f64(gate)[:1] * h
    return mxq(f64(w2), 0, "e4m3").T @ mxq(z, 0, "e4m3")

@@ -1,0 +1,156 @@
+from contextlib import ExitStack
+
+import concourse.mybir as mybir
+
+K, T, S, V, H, N = 512, 1024, 512, 1024, 512, 128
+P = 128
+
+F32 = mybir.dt.float32
+BF16 = mybir.dt.bfloat16
+U32 = mybir.dt.uint32
+U16 = mybir.dt.uint16
+U8 = mybir.dt.uint8
+FP8X4 = mybir.dt.float8_e4m3fn_x4
+RELU = mybir.ActivationFunctionType.Relu
+MULT = mybir.AluOpType.mult
+MAX = mybir.AluOpType.max
+
+FLOPS = 2 * H * K * S + 2 * N * H * V
+
+
+def tile_picked_voxel_relu_e_kernel(tc, xT, w1, w2, gate, offs, pos1, out):
+    nc = tc.nc
+    with ExitStack() as ctx:
+        held = ctx.enter_context(tc.tile_pool(name="held", bufs=1))
+        psum = ctx.enter_context(tc.psum_pool(name="psum", bufs=1))
+
+        points = held.tile([P, S // 16], U16, name="points")
+        cells = held.tile([P, S // 16], U16, name="cells")
+        nc.sync.dma_start(points[:], offs)
+
+        z = [held.tile([P, V], F32, name=f"z{t}") for t in range(4)]
+        warm = held.tile([P, 1], F32, name="warm")
+        warmed = held.tile([P, 1], F32, name="warmed")
+        nc.vector.memset(warm[:], 0.0)
+        nc.scalar.activation(warmed[:], warm[:], RELU)
+        nc.vector.memset(z[0][:], 0.0)
+        nc.gpsimd.memset(z[1][:], 0.0)
+        nc.vector.memset(z[2][:], 0.0)
+        nc.gpsimd.memset(z[3][:], 0.0)
+
+        xv = xT.rearrange("(p j) w -> p j w", j=4)
+        wv = w1.rearrange("(p j) w -> p j w", j=4)
+        TH = T // 2
+        xraw = {}
+        for u in range(2):
+            for a in range(2):
+                xraw[u, a] = held.tile([P, 2, TH], F32, name=f"xraw{u}{a}")
+                nc.sync.dma_start(xraw[u, a][:], xv[:, 2 * u : 2 * u + 2, a * TH : (a + 1) * TH])
+        HH = H // 2
+        wraw = []
+        for a in range(2):
+            wr = held.tile([P, 4, HH], F32, name=f"wraw{a}")
+            nc.sync.dma_start(wr[:], wv[:, :, a * HH : (a + 1) * HH])
+            wraw.append(wr)
+        nc.sync.dma_start(cells[:], pos1)
+        gates = held.tile([P, S], F32, name="gates")
+        nc.sync.dma_start(gates[:], gate)
+        w2raw = held.tile([P, 4, N], F32, name="w2raw")
+        nc.sync.dma_start(w2raw[:], w2.rearrange("(p j) n -> p j n", j=4))
+
+        pairs = [held.tile([P, T * 2], BF16, name=f"pairs{u}", align_bytes=64) for u in range(2)]
+        xg = held.tile([P, S * 4], BF16, name="xg", align_bytes=64)
+        xgw = xg[:].bitcast(U32).rearrange("p (n u) -> p n u", u=2)
+        xq = held.tile([P, S], U32, name="xq", align_bytes=64)
+        xs = held.tile([P, S], U8, name="xs", align_bytes=64)
+
+        def pair(copy, u, a, c0, c1):
+            dst = pairs[u][:].rearrange("p (w e) -> p w e", e=2)[:, a * TH + c0 : a * TH + c1, :]
+            copy(dst, xraw[u, a][:].rearrange("p e w -> p w e")[:, c0:c1, :])
+
+        w1g = held.tile([P, 4 * H], BF16, name="w1g", align_bytes=64)
+        w1q = held.tile([P, H], U32, name="w1q", align_bytes=64)
+        w1s = held.tile([P, H], U8, name="w1s", align_bytes=64)
+        MH = 64
+
+        def turn(copy, a, t0, t1):
+            if t1 - t0 == 1:
+                dst = w1g[:].rearrange("p (t m j) -> p t m j", t=4, j=4)[:, t0, a * MH : (a + 1) * MH, :]
+                src = wraw[a][:].rearrange("p j (m t) -> p t m j", t=4)[:, t0, :, :]
+            else:
+                dst = w1g[:].rearrange("p (t m j) -> p m t j", t=4, j=4)[:, a * MH : (a + 1) * MH, t0:t1, :]
+                src = wraw[a][:].rearrange("p j (m t) -> p m t j", t=4)[:, :, t0:t1, :]
+            copy(dst, src)
+
+        def quant_w1(c0, c1):
+            nc.vector.quantize_mx(
+                out=w1q[:, c0:c1].bitcast(FP8X4), scales=w1s[:, c0:c1], in_=w1g[:, 4 * c0 : 4 * c1]
+            )
+
+        vcopy, scopy = nc.vector.tensor_copy, nc.scalar.copy
+        pair(scopy, 0, 0, 0, TH)
+        pair(vcopy, 0, 1, 0, TH)
+        nc.vector.tensor_copy(xgw[:, :, 0], pairs[0][:].bitcast(U32).indirect(points[:]))
+        pair(scopy, 1, 0, 0, TH)
+        XC = 352
+        pair(vcopy, 1, 1, 0, XC)
+        pair(scopy, 1, 1, XC, TH)
+        nc.vector.tensor_copy(xgw[:, :, 1], pairs[1][:].bitcast(U32).indirect(points[:]))
+        turn(scopy, 0, 0, 1)
+        turn(scopy, 0, 1, 4)
+        nc.vector.quantize_mx(out=xq[:].bitcast(FP8X4), scales=xs[:], in_=xg[:])
+        turn(vcopy, 1, 0, 1)
+        turn(scopy, 1, 1, 4)
+        quant_w1(0, 128)
+
+        h = [psum.tile([P, S], F32, name=f"h{t}") for t in range(4)]
+        hr = [held.tile([P, S], F32, name=f"hr{t}") for t in range(4)]
+
+        def product(t):
+            cols = slice(128 * t, 128 * (t + 1))
+            nc.tensor.matmul_mx(
+                out=h[t][:], lhsT=w1q[:, cols].bitcast(FP8X4), lhsT_scale=w1s[:, cols],
+                rhs=xq[:].bitcast(FP8X4), rhs_scale=xs[:], start=True, stop=True,
+            )
+
+        zg = held.tile([P, V, 4], BF16, name="zg", align_bytes=64)
+        zq = held.tile([P, V], U32, name="zq", align_bytes=64)
+        zs = held.tile([P, V], U8, name="zs", align_bytes=64)
+
+        product(0)
+        quant_w1(128, 256)
+        quant_w1(256, 512)
+        for t in range(1, 4):
+            product(t)
+        w2g = held.tile([P, N * 4], BF16, name="w2g", align_bytes=64)
+        w2q = held.tile([P, N], U32, name="w2q", align_bytes=64)
+        w2s = held.tile([P, N], U8, name="w2s", align_bytes=64)
+        for t in range(4):
+            nc.scalar.activation(hr[t][:], h[t][:], RELU)
+        scopy(w2g[:].rearrange("p (n j) -> p n j", j=4), w2raw[:].rearrange("p j n -> p n j"))
+        for t in range(4):
+            nc.vector.tensor_tensor(z[t][:].indirect(cells[:]), hr[t][:], gates[:], MULT)
+            if t == 0:
+                nc.vector.quantize_mx(out=w2q[:].bitcast(FP8X4), scales=w2s[:], in_=w2g[:])
+            if t < 3:
+                scopy(zg[:, :, t], z[t][:])
+
+        VC = 640
+        nc.vector.tensor_copy(zg[:, 0:V:512, 3], zg[:, 0:V:512, 2])
+        vcopy(zg[:, 0:512, 3], z[3][:, 0:512])
+        scopy(zg[:, VC:V, 3], z[3][:, VC:V])
+        vcopy(zg[:, 512:VC, 3], z[3][:, 512:VC])
+        zgf = zg[:].rearrange("p v t -> p (v t)")
+
+        edges = [0, 512, 768, 1024]
+        for i in range(3):
+            c0, c1 = edges[i], edges[i + 1]
+            nc.vector.quantize_mx(out=zq[:, c0:c1].bitcast(FP8X4), scales=zs[:, c0:c1], in_=zgf[:, 4 * c0 : 4 * c1])
+            o = psum.tile([P, c1 - c0], F32, name=f"o{i}")
+            nc.tensor.matmul_mx(
+                out=o[:], lhsT=w2q[:].bitcast(FP8X4), lhsT_scale=w2s[:],
+                rhs=zq[:, c0:c1].bitcast(FP8X4), rhs_scale=zs[:, c0:c1], start=True, stop=True,
+            )
+            res = held.tile([P, c1 - c0], F32, name=f"res{i}")
+            (vcopy if i == 2 else scopy)(res[:], o[:])
+            nc.sync.dma_start(out[:, c0:c1], res[:])

@@ -13,20 +13,37 @@ U8 = mybir.dt.uint8
 FP8X4 = mybir.dt.float8_e4m3fn_x4
 RELU = mybir.ActivationFunctionType.Relu
 MULT = mybir.AluOpType.mult
-MAX = mybir.AluOpType.max
 
 FLOPS = 2 * H * K * S + 2 * N * H * V
 
 
 def tile_picked_voxel_relu_e_kernel(tc, xT, w1, w2, gate, offs, pos1, out):
     nc = tc.nc
+    vcopy, scopy = nc.vector.tensor_copy, nc.scalar.copy
     with ExitStack() as ctx:
         held = ctx.enter_context(tc.tile_pool(name="held", bufs=1))
         psum = ctx.enter_context(tc.psum_pool(name="psum", bufs=1))
 
         points = held.tile([P, S // 16], U16, name="points")
         cells = held.tile([P, S // 16], U16, name="cells")
+        gates = held.tile([P, S], F32, name="gates")
+        w2raw = held.tile([P, 4, N], F32, name="w2raw")
+        xv = xT.rearrange("(p j) w -> p j w", j=4)
+        wv = w1.rearrange("(p j) w -> p j w", j=4)
+
+        xraw = [held.tile([P, 2, T], F32, name=f"xraw{u}") for u in range(2)]
+        w1raw = held.tile([P, 4, H], F32, name="w1raw")
+        TH = T // 2
+        nc.sync.dma_start(xraw[0][:, :, 0:TH], xv[:, 0:2, 0:TH])
         nc.sync.dma_start(points[:], offs)
+        nc.sync.dma_start(xraw[0][:, :, TH:T], xv[:, 0:2, TH:T])
+        nc.sync.dma_start(xraw[1][:, :, 0:TH], xv[:, 2:4, 0:TH])
+        nc.sync.dma_start(xraw[1][:, :, TH:T], xv[:, 2:4, TH:T])
+        for b in range(2):
+            nc.sync.dma_start(w1raw[:, 2 * b : 2 * b + 2, :], wv[:, 2 * b : 2 * b + 2, :])
+        nc.sync.dma_start(cells[:], pos1)
+        nc.sync.dma_start(gates[:], gate)
+        nc.sync.dma_start(w2raw[:], w2.rearrange("(p j) n -> p j n", j=4))
 
         z = [held.tile([P, V], F32, name=f"z{t}") for t in range(4)]
         warm = held.tile([P, 1], F32, name="warm")
@@ -38,119 +55,110 @@ def tile_picked_voxel_relu_e_kernel(tc, xT, w1, w2, gate, offs, pos1, out):
         nc.vector.memset(z[2][:], 0.0)
         nc.gpsimd.memset(z[3][:], 0.0)
 
-        xv = xT.rearrange("(p j) w -> p j w", j=4)
-        wv = w1.rearrange("(p j) w -> p j w", j=4)
-        TH = T // 2
-        xraw = {}
-        for u in range(2):
-            for a in range(2):
-                xraw[u, a] = held.tile([P, 2, TH], F32, name=f"xraw{u}{a}")
-                nc.sync.dma_start(xraw[u, a][:], xv[:, 2 * u : 2 * u + 2, a * TH : (a + 1) * TH])
-        HH = H // 2
-        wraw = []
-        for a in range(2):
-            wr = held.tile([P, 4, HH], F32, name=f"wraw{a}")
-            nc.sync.dma_start(wr[:], wv[:, :, a * HH : (a + 1) * HH])
-            wraw.append(wr)
-        nc.sync.dma_start(cells[:], pos1)
-        gates = held.tile([P, S], F32, name="gates")
-        nc.sync.dma_start(gates[:], gate)
-        w2raw = held.tile([P, 4, N], F32, name="w2raw")
-        nc.sync.dma_start(w2raw[:], w2.rearrange("(p j) n -> p j n", j=4))
-
         pairs = [held.tile([P, T * 2], BF16, name=f"pairs{u}", align_bytes=64) for u in range(2)]
         xg = held.tile([P, S * 4], BF16, name="xg", align_bytes=64)
         xgw = xg[:].bitcast(U32).rearrange("p (n u) -> p n u", u=2)
         xq = held.tile([P, S], U32, name="xq", align_bytes=64)
         xs = held.tile([P, S], U8, name="xs", align_bytes=64)
-
-        def pair(copy, u, a, c0, c1):
-            dst = pairs[u][:].rearrange("p (w e) -> p w e", e=2)[:, a * TH + c0 : a * TH + c1, :]
-            copy(dst, xraw[u, a][:].rearrange("p e w -> p w e")[:, c0:c1, :])
-
         w1g = held.tile([P, 4 * H], BF16, name="w1g", align_bytes=64)
         w1q = held.tile([P, H], U32, name="w1q", align_bytes=64)
         w1s = held.tile([P, H], U8, name="w1s", align_bytes=64)
-        MH = 64
-
-        def turn(copy, a, t0, t1):
-            if t1 - t0 == 1:
-                dst = w1g[:].rearrange("p (t m j) -> p t m j", t=4, j=4)[:, t0, a * MH : (a + 1) * MH, :]
-                src = wraw[a][:].rearrange("p j (m t) -> p t m j", t=4)[:, t0, :, :]
-            else:
-                dst = w1g[:].rearrange("p (t m j) -> p m t j", t=4, j=4)[:, a * MH : (a + 1) * MH, t0:t1, :]
-                src = wraw[a][:].rearrange("p j (m t) -> p m t j", t=4)[:, :, t0:t1, :]
-            copy(dst, src)
-
-        def quant_w1(c0, c1):
-            nc.vector.quantize_mx(
-                out=w1q[:, c0:c1].bitcast(FP8X4), scales=w1s[:, c0:c1], in_=w1g[:, 4 * c0 : 4 * c1]
-            )
-
-        vcopy, scopy = nc.vector.tensor_copy, nc.scalar.copy
-        pair(scopy, 0, 0, 0, TH)
-        pair(vcopy, 0, 1, 0, TH)
-        nc.vector.tensor_copy(xgw[:, :, 0], pairs[0][:].bitcast(U32).indirect(points[:]))
-        pair(scopy, 1, 0, 0, TH)
-        XC = 352
-        pair(vcopy, 1, 1, 0, XC)
-        pair(scopy, 1, 1, XC, TH)
-        nc.vector.tensor_copy(xgw[:, :, 1], pairs[1][:].bitcast(U32).indirect(points[:]))
-        turn(scopy, 0, 0, 1)
-        turn(scopy, 0, 1, 4)
-        nc.vector.quantize_mx(out=xq[:].bitcast(FP8X4), scales=xs[:], in_=xg[:])
-        turn(vcopy, 1, 0, 1)
-        turn(scopy, 1, 1, 4)
-        quant_w1(0, 128)
-
-        h = [psum.tile([P, S], F32, name=f"h{t}") for t in range(4)]
+        w2q = held.tile([P, N], U32, name="w2q", align_bytes=64)
+        w2s = held.tile([P, N], U8, name="w2s", align_bytes=64)
         hr = [held.tile([P, S], F32, name=f"hr{t}") for t in range(4)]
-
-        def product(t):
-            cols = slice(128 * t, 128 * (t + 1))
-            nc.tensor.matmul_mx(
-                out=h[t][:], lhsT=w1q[:, cols].bitcast(FP8X4), lhsT_scale=w1s[:, cols],
-                rhs=xq[:].bitcast(FP8X4), rhs_scale=xs[:], start=True, stop=True,
-            )
-
         zg = held.tile([P, V, 4], BF16, name="zg", align_bytes=64)
         zq = held.tile([P, V], U32, name="zq", align_bytes=64)
         zs = held.tile([P, V], U8, name="zs", align_bytes=64)
 
-        product(0)
-        quant_w1(128, 256)
-        quant_w1(256, 512)
+        def pair(copy, u, c0, c1):
+            copy(
+                pairs[u][:].rearrange("p (w e) -> p w e", e=2)[:, c0:c1, :],
+                xraw[u][:].rearrange("p e w -> p w e")[:, c0:c1, :],
+            )
+
+        def pick(u, n0, n1):
+            nc.vector.tensor_copy(
+                xgw[:, n0:n1, u], pairs[u][:].bitcast(U32).indirect(points[:, n0 // 16 : n1 // 16])
+            )
+
+        def quantise(codes, scales, grouped, c0, c1):
+            nc.vector.quantize_mx(
+                out=codes[:, c0:c1].bitcast(FP8X4), scales=scales[:, c0:c1], in_=grouped[:, 4 * c0 : 4 * c1]
+            )
+
+        def turn(copy, j0, j1, t0, t1):
+            copy(
+                w1g[:].rearrange("p (t m j) -> p m t j", t=4, j=4)[:, :, t0:t1, j0:j1],
+                w1raw[:].rearrange("p j (m t) -> p m t j", t=4)[:, :, t0:t1, j0:j1],
+            )
+
+        def scatter(t, n0, n1):
+            nc.vector.tensor_tensor(
+                z[t][:].indirect(cells[:, n0 // 16 : n1 // 16]), hr[t][:, n0:n1], gates[:, n0:n1], MULT
+            )
+
+        def product(acc, t, n0, n1):
+            cols = slice(128 * t, 128 * (t + 1))
+            nc.tensor.matmul_mx(
+                out=acc[:], lhsT=w1q[:, cols].bitcast(FP8X4), lhsT_scale=w1s[:, cols],
+                rhs=xq[:, n0:n1].bitcast(FP8X4), rhs_scale=xs[:, n0:n1], start=True, stop=True,
+            )
+
+        pair(vcopy, 0, 0, TH)
+        pair(vcopy, 0, TH, T)
+        pick(0, 0, S)
+        pair(scopy, 1, 0, TH)
+        pair(vcopy, 1, TH, TH + 320)
+        pair(scopy, 1, TH + 320, T)
+        SH = S // 2
+        h0 = [psum.tile([P, SH], F32, name=f"h0{a}") for a in range(2)]
+        pick(1, 0, SH)
+        turn(scopy, 0, 2, 0, 1)
+        quantise(xq, xs, xg, 0, SH)
+        pick(1, SH, S)
+        turn(scopy, 2, 4, 0, 1)
+        quantise(w1q, w1s, w1g, 0, 128)
+        turn(scopy, 0, 4, 3, 4)
+        product(h0[0], 0, 0, SH)
+        nc.scalar.activation(hr[0][:, 0:SH], h0[0][:], RELU)
+        quantise(xq, xs, xg, SH, S)
+        product(h0[1], 0, SH, S)
+        nc.scalar.activation(hr[0][:, SH:S], h0[1][:], RELU)
+        turn(vcopy, 0, 4, 1, 3)
+        scatter(0, 0, SH)
+        scatter(0, SH, S)
+        quantise(w1q, w1s, w1g, 128, 256)
+        quantise(w1q, w1s, w1g, 256, 512)
         for t in range(1, 4):
-            product(t)
-        w2g = held.tile([P, N * 4], BF16, name="w2g", align_bytes=64)
-        w2q = held.tile([P, N], U32, name="w2q", align_bytes=64)
-        w2s = held.tile([P, N], U8, name="w2s", align_bytes=64)
-        for t in range(4):
-            nc.scalar.activation(hr[t][:], h[t][:], RELU)
+            ht = psum.tile([P, S], F32, name=f"h{t}")
+            product(ht, t, 0, S)
+            nc.scalar.activation(hr[t][:], ht[:], RELU)
+        w2g = held.tile([P, N * 4], BF16, name="w2g", tag="xg", align_bytes=64)
         scopy(w2g[:].rearrange("p (n j) -> p n j", j=4), w2raw[:].rearrange("p j n -> p n j"))
+
         for t in range(4):
-            nc.vector.tensor_tensor(z[t][:].indirect(cells[:]), hr[t][:], gates[:], MULT)
-            if t == 0:
-                nc.vector.quantize_mx(out=w2q[:].bitcast(FP8X4), scales=w2s[:], in_=w2g[:])
+            if t > 0:
+                scatter(t, 0, S)
+            if t == 1:
+                quantise(w2q, w2s, w2g, 0, N)
             if t < 3:
                 scopy(zg[:, :, t], z[t][:])
 
-        VC = 640
-        nc.vector.tensor_copy(zg[:, 0:V:512, 3], zg[:, 0:V:512, 2])
-        vcopy(zg[:, 0:512, 3], z[3][:, 0:512])
-        scopy(zg[:, VC:V, 3], z[3][:, VC:V])
-        vcopy(zg[:, 512:VC, 3], z[3][:, 512:VC])
+        nc.vector.tensor_copy(zg[:, 0:512:256, 3], zg[:, 0:512:256, 2])
+        for i in range(2):
+            vcopy(zg[:, 256 * i : 256 * i + 256, 3], z[3][:, 256 * i : 256 * i + 256])
+            scopy(zg[:, 512 + 256 * i : 768 + 256 * i, 3], z[3][:, 512 + 256 * i : 768 + 256 * i])
         zgf = zg[:].rearrange("p v t -> p (v t)")
 
-        edges = [0, 512, 768, 1024]
-        for i in range(3):
+        edges = [0, 256, 512, 768, 896, 1024]
+        for i in range(5):
             c0, c1 = edges[i], edges[i + 1]
-            nc.vector.quantize_mx(out=zq[:, c0:c1].bitcast(FP8X4), scales=zs[:, c0:c1], in_=zgf[:, 4 * c0 : 4 * c1])
-            o = psum.tile([P, c1 - c0], F32, name=f"o{i}")
+            quantise(zq, zs, zgf, c0, c1)
+            o = psum.tile([P, c1 - c0], F32, name=f"o{i}", tag=f"h0{i - 3}" if i > 2 else f"o{i}")
             nc.tensor.matmul_mx(
                 out=o[:], lhsT=w2q[:].bitcast(FP8X4), lhsT_scale=w2s[:],
                 rhs=zq[:, c0:c1].bitcast(FP8X4), rhs_scale=zs[:, c0:c1], start=True, stop=True,
             )
             res = held.tile([P, c1 - c0], F32, name=f"res{i}")
-            (vcopy if i == 2 else scopy)(res[:], o[:])
+            (vcopy if i == 4 else scopy)(res[:], o[:])
             nc.sync.dma_start(out[:, c0:c1], res[:])

@@ -118,13 +118,13 @@ def tile_picked_voxel_relu_e_kernel(tc, xT, w1, w2, gate, offs, pos1, out):
         pick(1, SH, S)
         turn(scopy, 2, 4, 0, 1)
         quantise(w1q, w1s, w1g, 0, 128)
-        turn(scopy, 0, 4, 3, 4)
+        turn(scopy, 0, 4, 1, 3)
         product(h0[0], 0, 0, SH)
         nc.scalar.activation(hr[0][:, 0:SH], h0[0][:], RELU)
         quantise(xq, xs, xg, SH, S)
         product(h0[1], 0, SH, S)
         nc.scalar.activation(hr[0][:, SH:S], h0[1][:], RELU)
-        turn(vcopy, 0, 4, 1, 3)
+        turn(vcopy, 0, 4, 3, 4)
         scatter(0, 0, SH)
         scatter(0, SH, S)
         quantise(w1q, w1s, w1g, 128, 256)

from contextlib import ExitStack

import concourse.mybir as mybir

K, T, S, V, H, N = 512, 1024, 512, 1024, 512, 128
P = 128

F32 = mybir.dt.float32
BF16 = mybir.dt.bfloat16
U32 = mybir.dt.uint32
U16 = mybir.dt.uint16
U8 = mybir.dt.uint8
FP8X4 = mybir.dt.float8_e4m3fn_x4
RELU = mybir.ActivationFunctionType.Relu
MULT = mybir.AluOpType.mult

FLOPS = 2 * H * K * S + 2 * N * H * V


def tile_picked_voxel_relu_e_kernel(tc, xT, w1, w2, gate, offs, pos1, out):
    nc = tc.nc
    vcopy, scopy = nc.vector.tensor_copy, nc.scalar.copy
    with ExitStack() as ctx:
        held = ctx.enter_context(tc.tile_pool(name="held", bufs=1))
        psum = ctx.enter_context(tc.psum_pool(name="psum", bufs=1))

        points = held.tile([P, S // 16], U16, name="points")
        cells = held.tile([P, S // 16], U16, name="cells")
        gates = held.tile([P, S], F32, name="gates")
        w2raw = held.tile([P, 4, N], F32, name="w2raw")
        xv = xT.rearrange("(p j) w -> p j w", j=4)
        wv = w1.rearrange("(p j) w -> p j w", j=4)

        xraw = [held.tile([P, 2, T], F32, name=f"xraw{u}") for u in range(2)]
        w1raw = held.tile([P, 4, H], F32, name="w1raw")
        TH = T // 2
        nc.sync.dma_start(xraw[0][:, :, 0:TH], xv[:, 0:2, 0:TH])
        nc.sync.dma_start(points[:], offs)
        nc.sync.dma_start(xraw[0][:, :, TH:T], xv[:, 0:2, TH:T])
        nc.sync.dma_start(xraw[1][:, :, 0:TH], xv[:, 2:4, 0:TH])
        nc.sync.dma_start(xraw[1][:, :, TH:T], xv[:, 2:4, TH:T])
        for b in range(2):
            nc.sync.dma_start(w1raw[:, 2 * b : 2 * b + 2, :], wv[:, 2 * b : 2 * b + 2, :])
        nc.sync.dma_start(cells[:], pos1)
        nc.sync.dma_start(gates[:], gate)
        nc.sync.dma_start(w2raw[:], w2.rearrange("(p j) n -> p j n", j=4))

        z = [held.tile([P, V], F32, name=f"z{t}") for t in range(4)]
        warm = held.tile([P, 1], F32, name="warm")
        warmed = held.tile([P, 1], F32, name="warmed")
        nc.vector.memset(warm[:], 0.0)
        nc.scalar.activation(warmed[:], warm[:], RELU)
        nc.vector.memset(z[0][:], 0.0)
        nc.gpsimd.memset(z[1][:], 0.0)
        nc.vector.memset(z[2][:], 0.0)
        nc.gpsimd.memset(z[3][:], 0.0)

        pairs = [held.tile([P, T * 2], BF16, name=f"pairs{u}", align_bytes=64) for u in range(2)]
        xg = held.tile([P, S * 4], BF16, name="xg", align_bytes=64)
        xgw = xg[:].bitcast(U32).rearrange("p (n u) -> p n u", u=2)
        xq = held.tile([P, S], U32, name="xq", align_bytes=64)
        xs = held.tile([P, S], U8, name="xs", align_bytes=64)
        w1g = held.tile([P, 4 * H], BF16, name="w1g", align_bytes=64)
        w1q = held.tile([P, H], U32, name="w1q", align_bytes=64)
        w1s = held.tile([P, H], U8, name="w1s", align_bytes=64)
        w2q = held.tile([P, N], U32, name="w2q", align_bytes=64)
        w2s = held.tile([P, N], U8, name="w2s", align_bytes=64)
        hr = [held.tile([P, S], F32, name=f"hr{t}") for t in range(4)]
        zg = held.tile([P, V, 4], BF16, name="zg", align_bytes=64)
        zq = held.tile([P, V], U32, name="zq", align_bytes=64)
        zs = held.tile([P, V], U8, name="zs", align_bytes=64)

        def pair(copy, u, c0, c1):
            copy(
                pairs[u][:].rearrange("p (w e) -> p w e", e=2)[:, c0:c1, :],
                xraw[u][:].rearrange("p e w -> p w e")[:, c0:c1, :],
            )

        def pick(u, n0, n1):
            nc.vector.tensor_copy(
                xgw[:, n0:n1, u], pairs[u][:].bitcast(U32).indirect(points[:, n0 // 16 : n1 // 16])
            )

        def quantise(codes, scales, grouped, c0, c1):
            nc.vector.quantize_mx(
                out=codes[:, c0:c1].bitcast(FP8X4), scales=scales[:, c0:c1], in_=grouped[:, 4 * c0 : 4 * c1]
            )

        def turn(copy, j0, j1, t0, t1):
            copy(
                w1g[:].rearrange("p (t m j) -> p m t j", t=4, j=4)[:, :, t0:t1, j0:j1],
                w1raw[:].rearrange("p j (m t) -> p m t j", t=4)[:, :, t0:t1, j0:j1],
            )

        def scatter(t, n0, n1):
            nc.vector.tensor_tensor(
                z[t][:].indirect(cells[:, n0 // 16 : n1 // 16]), hr[t][:, n0:n1], gates[:, n0:n1], MULT
            )

        def product(acc, t, n0, n1):
            cols = slice(128 * t, 128 * (t + 1))
            nc.tensor.matmul_mx(
                out=acc[:], lhsT=w1q[:, cols].bitcast(FP8X4), lhsT_scale=w1s[:, cols],
                rhs=xq[:, n0:n1].bitcast(FP8X4), rhs_scale=xs[:, n0:n1], start=True, stop=True,
            )

        pair(vcopy, 0, 0, TH)
        pair(vcopy, 0, TH, T)
        pick(0, 0, S)
        pair(scopy, 1, 0, TH)
        pair(vcopy, 1, TH, TH + 320)
        pair(scopy, 1, TH + 320, T)
        SH = S // 2
        h0 = [psum.tile([P, SH], F32, name=f"h0{a}") for a in range(2)]
        pick(1, 0, SH)
        turn(scopy, 0, 2, 0, 1)
        quantise(xq, xs, xg, 0, SH)
        pick(1, SH, S)
        turn(scopy, 2, 4, 0, 1)
        quantise(w1q, w1s, w1g, 0, 128)
        turn(scopy, 0, 4, 1, 3)
        product(h0[0], 0, 0, SH)
        nc.scalar.activation(hr[0][:, 0:SH], h0[0][:], RELU)
        quantise(xq, xs, xg, SH, S)
        product(h0[1], 0, SH, S)
        nc.scalar.activation(hr[0][:, SH:S], h0[1][:], RELU)
        turn(vcopy, 0, 4, 3, 4)
        scatter(0, 0, SH)
        scatter(0, SH, S)
        quantise(w1q, w1s, w1g, 128, 256)
        quantise(w1q, w1s, w1g, 256, 512)
        for t in range(1, 4):
            ht = psum.tile([P, S], F32, name=f"h{t}")
            product(ht, t, 0, S)
            nc.scalar.activation(hr[t][:], ht[:], RELU)
        w2g = held.tile([P, N * 4], BF16, name="w2g", tag="xg", align_bytes=64)
        scopy(w2g[:].rearrange("p (n j) -> p n j", j=4), w2raw[:].rearrange("p j n -> p n j"))

        for t in range(4):
            if t > 0:
                scatter(t, 0, S)
            if t == 1:
                quantise(w2q, w2s, w2g, 0, N)
            if t < 3:
                scopy(zg[:, :, t], z[t][:])

        nc.vector.tensor_copy(zg[:, 0:512:256, 3], zg[:, 0:512:256, 2])
        for i in range(2):
            vcopy(zg[:, 256 * i : 256 * i + 256, 3], z[3][:, 256 * i : 256 * i + 256])
            scopy(zg[:, 512 + 256 * i : 768 + 256 * i, 3], z[3][:, 512 + 256 * i : 768 + 256 * i])
        zgf = zg[:].rearrange("p v t -> p (v t)")

        edges = [0, 256, 512, 768, 896, 1024]
        for i in range(5):
            c0, c1 = edges[i], edges[i + 1]
            quantise(zq, zs, zgf, c0, c1)
            o = psum.tile([P, c1 - c0], F32, name=f"o{i}", tag=f"h0{i - 3}" if i > 2 else f"o{i}")
            nc.tensor.matmul_mx(
                out=o[:], lhsT=w2q[:].bitcast(FP8X4), lhsT_scale=w2s[:],
                rhs=zq[:, c0:c1].bitcast(FP8X4), rhs_scale=zs[:, c0:c1], start=True, stop=True,
            )
            res = held.tile([P, c1 - c0], F32, name=f"res{i}")
            (vcopy if i == 4 else scopy)(res[:], o[:])
            nc.sync.dma_start(out[:, c0:c1], res[:])
